import numpy as np
import ml_dtypes


def mxq(x, axis, fmt="e4m3"):
    dtype, down = {"e4m3": (ml_dtypes.float8_e4m3fn, 7), "e5m2": (ml_dtypes.float8_e5m2, 14)}[fmt]
    v = np.moveaxis(np.asarray(x, np.float32).astype(ml_dtypes.bfloat16).astype(np.float64), axis, -1)
    blocks = v.reshape(v.shape[:-1] + (-1, 32))
    amax = np.abs(blocks).max(-1, keepdims=True)
    byte = np.maximum(np.where(amax > 0, np.frexp(amax)[1] - 1 + 127, 0) - down, 1)
    scale = np.exp2(byte - 127.0)
    codes = (blocks / scale).astype(np.float32).astype(dtype).astype(np.float64)
    return np.moveaxis((codes * scale).reshape(v.shape), -1, axis)


WIDE = False


def mx_kscale(k):
    if not WIDE:
        return np.ones(k)
    levels = np.array([10, -10, 5, -5, 0])
    if k % 512:
        return np.exp2(np.random.permutation(np.resize(levels, k // 32))).repeat(32)
    a = np.empty((k // 512, 16))
    for p in range(k // 512):
        a[p, :8] = np.random.permutation(np.resize(levels, 8))
        for g in range(8):
            far = levels[np.abs(levels - a[p, g]) >= 10]
            a[p, g + 8] = far[np.random.randint(len(far))]
    return np.exp2(a.ravel()).repeat(32)


def f64(x):
    return np.asarray(x).astype(np.float64)


def striped(idx):
    return np.tile(np.asarray(idx).reshape(-1, 16).T, (8, 1)).astype(np.uint16)


def unstriped(offs):
    return offs[:16].T.reshape(-1).astype(np.int64)


def striped8(idx):
    return np.asarray(idx).reshape(8, -1, 16).transpose(0, 2, 1).reshape(128, -1).astype(np.uint16)


def unstriped8(offs):
    return offs.reshape(8, 16, -1).transpose(0, 2, 1).reshape(8, -1).astype(np.int64)


def pick8(x, idx, run):
    r = np.arange(len(x))
    return x[r[:, None], idx[r % (8 * run) // run]]


E2M1 = np.array([0.0, 0.5, 1.0, 1.5, 2.0, 3.0, 4.0, 6.0, -0.0, -0.5, -1.0, -1.5, -2.0, -3.0, -4.0, -6.0])


def pack_weight(w, fmt):
    k, n = w.shape
    w = f64(np.asarray(w, np.float32).astype(ml_dtypes.bfloat16)).reshape(k // 32, 32, n)
    amax = np.abs(w).max(1)
    if fmt == "e4m3":
        byte = np.frexp(amax)[1] - 1 + 127 - 7
    else:
        mant, ex = np.frexp(amax / 6.0)
        byte = np.where(mant > 0.5, ex, ex - 1) + 127
    byte = np.clip(np.where(amax > 0, byte, 1), 1, 254)
    scaled = (w * np.exp2(127.0 - byte)[:, None, :]).reshape(k, n).astype(np.float32)
    by_word = np.ascontiguousarray(scaled.reshape(k // 512, 128, 4, n).transpose(0, 1, 3, 2))
    if fmt == "e4m3":
        words = by_word.astype(ml_dtypes.float8_e4m3fn).view(np.uint8)
    else:
        c = by_word.astype(ml_dtypes.float4_e2m1fn).view(np.uint8) & 0xF
        words = (c[..., 0::2] | (c[..., 1::2] << 4)).reshape(k // 512, 128, 2 * n)
    return np.ascontiguousarray(words), np.ascontiguousarray(byte.astype(np.uint8).reshape(k // 512, 16, n))


def unpack_weight(words, scales, fmt):
    g, _, n = scales.shape
    words = np.ascontiguousarray(words).reshape(g, 128, n, -1)
    if fmt == "e4m3":
        vals = words.view(ml_dtypes.float8_e4m3fn).astype(np.float64)
    else:
        nib = np.empty((g, 128, n, 4), np.uint8)
        nib[..., 0::2] = words & 0xF
        nib[..., 1::2] = words >> 4
        vals = E2M1[nib]
    vals = vals * np.repeat(np.exp2(scales.astype(np.float64) - 127.0), 8, axis=1)[..., None]
    return vals.transpose(0, 1, 3, 2).reshape(g * 512, n)


def sigmoid(v):
    return 1.0 / (1.0 + np.exp(-v))


def bf(x):
    return np.asarray(x, np.float32).astype(ml_dtypes.bfloat16)


def planes(Y):
    r, m = Y.shape
    b = f64(bf(Y)).reshape(r // 32, 32, m)
    amax = np.abs(b).max(1)
    byte = np.clip(np.where(amax > 0, np.frexp(amax)[1] - 1 + 127 - 7, 1), 1, 254)
    codes = (b * np.exp2(127.0 - byte)[:, None, :]).reshape(r, m).astype(np.float32).astype(ml_dtypes.float8_e4m3fn).view(np.uint8)
    words = codes.reshape(r // 512, 128, 4, m).transpose(0, 1, 3, 2)
    return np.ascontiguousarray(words), np.ascontiguousarray(byte.astype(np.uint8).reshape(r // 512, 16, m))


K, R, F, T, J, M = 512, 512, 512, 2048, 512, 128


def setup_inputs():
    n = np.random.standard_normal
    idx = np.random.permutation(T)[:J]
    idx2 = np.stack([np.random.permutation(J)[:M] for _ in range(8)])
    idx3 = np.stack([np.random.permutation(J)[:M] for _ in range(8)])
    fk = mx_kscale(K)
    fr = mx_kscale(R)
    tabp = pack_weight(n((K, T)) / fk[:, None], "e2m1")
    return {
        "tab_words": tabp[0],
        "tab_scales": tabp[1],
        "w1": (n((K, R)) * 1 / np.sqrt(K) * fk[:, None]).astype(np.float32),
        "gain": (np.random.uniform(0.5, 1.5, (R, 1))).astype(np.float32),
        "steep": (np.random.uniform(0.7, 2.5, (R, 1))).astype(np.float32),
        "rs": (np.random.uniform(0.5, 2.0, (R, 1)) * fr[:, None]).astype(np.float32),
        "wor": (n((R, F)) * 1 / np.sqrt(R) / fr[:, None]).astype(np.float32),
        "res": (n((F, M)) * 0.5).astype(np.float32),
        "offs": striped(idx),
        "offs2": striped8(idx2),
        "offs3": striped8(idx3),
    }


def reference(tab_words, tab_scales, w1, gain, steep, rs, wor, res, offs, offs2, offs3):
    idx = unstriped(offs)
    idx2 = unstriped8(offs2)
    idx3 = unstriped8(offs3)
    tabu = unpack_weight(tab_words, tab_scales, "e2m1")
    w1q = mxq(f64(w1), 0, "e4m3")
    tabidxg = tabu[:, idx]
    a = w1q.T @ tabidxg
    h1 = a * f64(gain)
    gt = sigmoid((pick8(h1, idx2, 64) - pick8(h1, idx3, 64)) * f64(steep))
    u1 = pick8(h1, idx3, 64) + (pick8(h1, idx2, 64) - pick8(h1, idx3, 64)) * gt
    fo1 = u1 * f64(rs)
    worq = mxq(f64(wor), 0, "e4m3")
    fo1q = mxq(fo1, 0, "e4m3")
    yo = worq.T @ fo1q
    y = yo + f64(res)
    words, scales = planes(y)
    return y, words, scales

@@ -1,0 +1,159 @@
+from contextlib import ExitStack
+
+import concourse.mybir as mybir
+
+K, R, F, T, J, M = 512, 512, 512, 2048, 512, 128
+FLOPS = 2 * K * R * J + 2 * R * F * M
+
+F32 = mybir.dt.float32
+BF16 = mybir.dt.bfloat16
+I32 = mybir.dt.int32
+U32 = mybir.dt.uint32
+U16 = mybir.dt.uint16
+U8 = mybir.dt.uint8
+FP8X4 = mybir.dt.float8_e4m3fn_x4
+FP4X4 = mybir.dt.float4_e2m1fn_x4
+ACT = mybir.ActivationFunctionType
+ALU = mybir.AluOpType
+
+P = 128
+PACK = 4
+QUADS = 4
+
+
+def deal(copy, grouped, raw, m0, m1, r0):
+    copy(
+        out=grouped[:, :, m0:m1, :].rearrange("p t m j -> p m j t"),
+        in_=raw[:, :, PACK * (m0 - r0) : PACK * (m1 - r0)].rearrange("p j (m t) -> p m j t", t=PACK),
+    )
+
+
+def tile_attend_chsoftlarger_pl_kernel(tc, tab_words, tab_scales, w1, gain, steep, rs, wor, res, offs, offs2, offs3, out_0, out_1, out_2):
+    nc = tc.nc
+    with ExitStack() as ctx:
+        sb = ctx.enter_context(tc.tile_pool(name="sb", bufs=1))
+        ps = ctx.enter_context(tc.psum_pool(name="ps", bufs=1))
+
+        slots = sb.tile([P, J // 16], U16, name="slots")
+        picks2 = sb.tile([P, M // 16], U16, name="picks2")
+        picks3 = sb.tile([P, M // 16], U16, name="picks3")
+        words = sb.tile([P, T], U16, name="words", align_bytes=64)
+        tscales = sb.tile([P, T], U8, name="tscales", align_bytes=64)
+
+        nc.vector.memset(tscales[:].bitcast(I32), 0)
+        warm = sb.tile([P, 1], F32, name="warm")
+        warm_out = sb.tile([P, 1], F32, name="warm_out")
+        nc.vector.memset(warm[:], 0.0)
+        nc.scalar.activation(warm_out[:], warm[:], ACT.Sigmoid)
+
+        nc.sync.dma_start(slots[:], offs)
+        nc.sync.dma_start(words[:].bitcast(I32), tab_words[0].bitcast(I32))
+        for q in range(QUADS):
+            nc.sync.dma_start(tscales[32 * q : 32 * q + 4, :].bitcast(I32), tab_scales[0, 4 * q : 4 * q + 4, :].bitcast(I32))
+        w1_rows = w1.rearrange("(p j) r -> p j r", j=PACK)
+        w1_raw = []
+        for c in range(2):
+            raw = sb.tile([P, PACK, R // 2], F32, name="w1_raw%d" % c)
+            nc.sync.dma_start(raw[:], w1_rows[:, :, c * (R // 2) : (c + 1) * (R // 2)])
+            w1_raw.append(raw)
+        gain_sb = sb.tile([P, PACK], F32, name="gain_sb")
+        steep_sb = sb.tile([P, PACK], F32, name="steep_sb")
+        rs_sb = sb.tile([P, PACK], F32, name="rs_sb")
+        nc.sync.dma_start(gain_sb[:], gain.rearrange("(p t) o -> p (t o)", t=PACK))
+        nc.sync.dma_start(picks3[:], offs3)
+        nc.sync.dma_start(picks2[:], offs2)
+        nc.sync.dma_start(steep_sb[:], steep.rearrange("(p t) o -> p (t o)", t=PACK))
+        nc.sync.dma_start(rs_sb[:], rs.rearrange("(p t) o -> p (t o)", t=PACK))
+        wor_rows = wor.rearrange("(p j) f -> p j f", j=PACK)
+        wor_raw = []
+        for c in range(2):
+            raw = sb.tile([P, PACK, F // 2], F32, name="wor_raw%d" % c)
+            nc.sync.dma_start(raw[:], wor_rows[:, :, c * (F // 2) : (c + 1) * (F // 2)])
+            wor_raw.append(raw)
+        res_sb = sb.tile([P, PACK, M], F32, name="res_sb")
+        nc.sync.dma_start(res_sb[:], res.rearrange("(p t) m -> p t m", t=PACK))
+
+        gwords = sb.tile([P, J], U16, name="gwords", align_bytes=64)
+        gscales = sb.tile([P, J], U8, name="gscales", align_bytes=64)
+        nc.vector.tensor_copy(gwords[:], words[:].indirect(slots[:]))
+        nc.vector.tensor_copy(gscales[:], tscales[:].indirect(slots[:]))
+
+        w1_bf = sb.tile([P, PACK, P, PACK], BF16, name="w1_bf", align_bytes=64)
+        deal(nc.scalar.copy, w1_bf, w1_raw[0], 0, 44, 0)
+        deal(nc.vector.tensor_copy, w1_bf, w1_raw[0], 44, 64, 0)
+        deal(nc.vector.tensor_copy, w1_bf, w1_raw[1], 64, 108, 64)
+        deal(nc.scalar.copy, w1_bf, w1_raw[1], 108, 128, 64)
+
+        h1 = []
+        for t in range(PACK):
+            codes = sb.tile([P, P], U32, name="w1_codes%d" % t, align_bytes=64)
+            scales = sb.tile([P, P], U8, name="w1_scales%d" % t, align_bytes=64)
+            nc.vector.quantize_mx(out=codes[:].bitcast(FP8X4), scales=scales[:], in_=w1_bf[:, t, :, :].rearrange("p m j -> p (m j)"))
+            acc = ps.tile([P, J], F32, name="acc%d" % t)
+            nc.tensor.matmul_mx(out=acc[:], lhsT=codes[:].bitcast(FP8X4), lhsT_scale=scales[:], rhs=gwords[:].bitcast(FP4X4), rhs_scale=gscales[:], start=True, stop=True)
+            h = sb.tile([P, J], F32, name="h1_%d" % t)
+            nc.scalar.activation(h[:], acc[:], ACT.Copy, scale=gain_sb[:, t : t + 1])
+            h1.append(h)
+
+        wor_bf = sb.tile([P, PACK, P, PACK], BF16, name="wor_bf", align_bytes=64)
+        wor_codes = sb.tile([P, PACK, P], U32, name="wor_codes", align_bytes=64)
+        wor_scales = sb.tile([P, PACK, P], U8, name="wor_scales", align_bytes=64)
+
+        def quantize_wor(c):
+            half = slice(64 * c, 64 * (c + 1))
+            for t in range(PACK):
+                nc.vector.quantize_mx(out=wor_codes[:, t, half].bitcast(FP8X4), scales=wor_scales[:, t, half], in_=wor_bf[:, t, half, :].rearrange("p m j -> p (m j)"))
+
+        deal(nc.vector.tensor_copy, wor_bf, wor_raw[0], 0, 64, 0)
+        quantize_wor(0)
+
+        base = sb.tile([P, PACK, M], F32, name="base")
+        base_rs = sb.tile([P, PACK, M], F32, name="base_rs")
+        diff = sb.tile([P, PACK, M], F32, name="diff")
+        gate = sb.tile([P, PACK, M], F32, name="gate")
+        step = sb.tile([P, PACK, M], F32, name="step")
+        for t in range(PACK):
+            nc.vector.tensor_copy(base[:, t, :], h1[t][:].indirect(picks3[:]))
+            nc.vector.tensor_tensor(diff[:, t, :], h1[t][:].indirect(picks2[:]), base[:, t, :], ALU.subtract)
+            nc.scalar.activation(gate[:, t, :], diff[:, t, :], ACT.Sigmoid, scale=steep_sb[:, t : t + 1])
+            nc.scalar.activation(base_rs[:, t, :], base[:, t, :], ACT.Copy, scale=rs_sb[:, t : t + 1])
+            nc.vector.scalar_tensor_tensor(step[:, t, :], diff[:, t, :], rs_sb[:, t : t + 1], gate[:, t, :], ALU.mult, ALU.mult)
+
+        deal(nc.scalar.copy, wor_bf, wor_raw[1], 64, 96, 64)
+        deal(nc.scalar.copy, wor_bf, wor_raw[1], 96, 128, 64)
+        quantize_wor(1)
+
+        fo_bf = sb.tile([P, M, PACK], BF16, name="fo_bf", align_bytes=64)
+        nc.vector.tensor_tensor(
+            fo_bf[:].rearrange("p (c i) t -> p c t i", i=4),
+            step[:].rearrange("p t (c i) -> p c t i", i=4),
+            base_rs[:].rearrange("p t (c i) -> p c t i", i=4),
+            ALU.add,
+        )
+        fo_codes = sb.tile([P, M], U32, name="fo_codes", align_bytes=64)
+        fo_scales = sb.tile([P, M], U8, name="fo_scales", align_bytes=64)
+        nc.vector.quantize_mx(out=fo_codes[:].bitcast(FP8X4), scales=fo_scales[:], in_=fo_bf[:].rearrange("p m t -> p (m t)"))
+
+        y = sb.tile([P, PACK, M], F32, name="y")
+        out_rows = out_0.rearrange("(p t) m -> p t m", t=PACK)
+        for u in range(2):
+            pair = slice(2 * u, 2 * u + 2)
+            yo = ps.tile([P, 2, M], F32, name="yo%d" % u)
+            for e in range(2):
+                t = 2 * u + e
+                nc.tensor.matmul_mx(out=yo[:, e, :], lhsT=wor_codes[:, t, :].bitcast(FP8X4), lhsT_scale=wor_scales[:, t, :], rhs=fo_codes[:].bitcast(FP8X4), rhs_scale=fo_scales[:], start=True, stop=True)
+            nc.vector.tensor_tensor(y[:, pair, :], yo[:], res_sb[:, pair, :], ALU.add)
+            nc.sync.dma_start(out_rows[:, pair, :], y[:, pair, :])
+
+        y_bf = sb.tile([P, M, PACK], BF16, name="y_bf", align_bytes=64)
+        y_codes = sb.tile([P, M], U32, name="y_codes", align_bytes=64)
+        y_scales = sb.tile([P, M], U8, name="y_scales", align_bytes=64)
+        halves = [slice(0, M // 2), slice(M // 2, M)]
+        for half in halves:
+            nc.vector.tensor_copy(y_bf[:, half, :].rearrange("p (c i) t -> p c t i", i=4), y[:, :, half].rearrange("p t (c i) -> p c t i", i=4))
+        for half in halves:
+            nc.vector.quantize_mx(out=y_codes[:, half].bitcast(FP8X4), scales=y_scales[:, half], in_=y_bf[:, half, :].rearrange("p m t -> p (m t)"))
+        nc.scalar.dma_start(out_1[0].rearrange("p c r -> p (c r)").bitcast(I32), y_codes[:].bitcast(I32))
+        for q in range(QUADS):
+            queue = nc.sync if q % 2 == 0 else nc.scalar
+            queue.dma_start(out_2[0, 4 * q : 4 * q + 4, :].bitcast(I32), y_scales[32 * q : 32 * q + 4, :].bitcast(I32))

@@ -19,12 +19,13 @@ ALU = mybir.AluOpType
 P = 128
 PACK = 4
 QUADS = 4
+WA = 64
 
 
-def deal(copy, grouped, raw, m0, m1, r0):
+def deal(copy, grouped, raw, u, m0, m1):
     copy(
-        out=grouped[:, :, m0:m1, :].rearrange("p t m j -> p m j t"),
-        in_=raw[:, :, PACK * (m0 - r0) : PACK * (m1 - r0)].rearrange("p j (m t) -> p m j t", t=PACK),
+        out=grouped[:, :, m0:m1, :].rearrange("p e m j -> p m j e"),
+        in_=raw[:].rearrange("p j (m t) -> p m j t", t=PACK)[:, :, :, 2 * u : 2 * u + 2],
     )
 
 
@@ -57,20 +58,19 @@ def tile_attend_chsoftlarger_pl_kernel(tc, tab_words, tab_scales, w1, gain, stee
             nc.sync.dma_start(raw[:], w1_rows[:, :, c * (R // 2) : (c + 1) * (R // 2)])
             w1_raw.append(raw)
         gain_sb = sb.tile([P, PACK], F32, name="gain_sb")
-        steep_sb = sb.tile([P, PACK], F32, name="steep_sb")
+        steep_sb = sb.tile([P, PACK], F32, name="steep_sb", tag="after_gates", align_bytes=64)
         rs_sb = sb.tile([P, PACK], F32, name="rs_sb")
+        wor_rows = wor.rearrange("(p j) f -> p j f", j=PACK)
+        wor_a = sb.tile([P, PACK, PACK * WA], F32, name="wor_a", tag="after_wor_a")
+        wor_b = sb.tile([P, PACK, F - PACK * WA], F32, name="wor_b")
+        res_sb = sb.tile([P, PACK, M], F32, name="res_sb")
         nc.sync.dma_start(gain_sb[:], gain.rearrange("(p t) o -> p (t o)", t=PACK))
         nc.sync.dma_start(picks3[:], offs3)
         nc.sync.dma_start(picks2[:], offs2)
         nc.sync.dma_start(steep_sb[:], steep.rearrange("(p t) o -> p (t o)", t=PACK))
         nc.sync.dma_start(rs_sb[:], rs.rearrange("(p t) o -> p (t o)", t=PACK))
-        wor_rows = wor.rearrange("(p j) f -> p j f", j=PACK)
-        wor_raw = []
-        for c in range(2):
-            raw = sb.tile([P, PACK, F // 2], F32, name="wor_raw%d" % c)
-            nc.sync.dma_start(raw[:], wor_rows[:, :, c * (F // 2) : (c + 1) * (F // 2)])
-            wor_raw.append(raw)
-        res_sb = sb.tile([P, PACK, M], F32, name="res_sb")
+        nc.sync.dma_start(wor_a[:], wor_rows[:, :, : PACK * WA])
+        nc.sync.dma_start(wor_b[:], wor_rows[:, :, PACK * WA :])
         nc.sync.dma_start(res_sb[:], res.rearrange("(p t) m -> p t m", t=PACK))
 
         gwords = sb.tile([P, J], U16, name="gwords", align_bytes=64)
@@ -78,51 +78,77 @@ def tile_attend_chsoftlarger_pl_kernel(tc, tab_words, tab_scales, w1, gain, stee
         nc.vector.tensor_copy(gwords[:], words[:].indirect(slots[:]))
         nc.vector.tensor_copy(gscales[:], tscales[:].indirect(slots[:]))
 
-        w1_bf = sb.tile([P, PACK, P, PACK], BF16, name="w1_bf", align_bytes=64)
-        deal(nc.scalar.copy, w1_bf, w1_raw[0], 0, 44, 0)
-        deal(nc.vector.tensor_copy, w1_bf, w1_raw[0], 44, 64, 0)
-        deal(nc.vector.tensor_copy, w1_bf, w1_raw[1], 64, 108, 64)
-        deal(nc.scalar.copy, w1_bf, w1_raw[1], 108, 128, 64)
+        base_rs = sb.tile([P, PACK, M], F32, name="base_rs")
+        diff = [sb.tile([P, M], F32, name="diff%d" % t) for t in range(PACK)]
+        step = sb.tile([P, PACK, M], F32, name="step", tag="after_mix", align_bytes=64)
 
+        w1_bf = [sb.tile([P, 2, P, PACK], BF16, name="w1_bf%d" % u, align_bytes=64) for u in range(2)]
+        w1_codes = sb.tile([P, PACK, P], U32, name="w1_codes", align_bytes=64)
+        w1_scales = sb.tile([P, PACK, P], U8, name="w1_scales", align_bytes=64)
+        deal(nc.scalar.copy, w1_bf[0], w1_raw[0], 0, 0, 64)
+        deal(nc.scalar.copy, w1_bf[1], w1_raw[0], 1, 0, 64)
+        deal(nc.vector.tensor_copy, w1_bf[0], w1_raw[1], 0, 64, 128)
+        deal(nc.scalar.copy, w1_bf[1], w1_raw[1], 1, 64, 128)
+
+        accs = []
+        for t in range(PACK):
+            nc.vector.quantize_mx(out=w1_codes[:, t, :].bitcast(FP8X4), scales=w1_scales[:, t, :], in_=w1_bf[t // 2][:, t % 2, :, :].rearrange("p m j -> p (m j)"))
+            acc = ps.tile([P, J], F32, name="acc%d" % t)
+            nc.tensor.matmul_mx(out=acc[:], lhsT=w1_codes[:, t, :].bitcast(FP8X4), lhsT_scale=w1_scales[:, t, :], rhs=gwords[:].bitcast(FP4X4), rhs_scale=gscales[:], start=True, stop=True)
+            accs.append(acc)
+
+        wor_bf = [sb.tile([P, 2, P, PACK], BF16, name="wor_bf%d" % u, align_bytes=64) for u in range(2)]
+        for u in range(2):
+            deal(nc.vector.tensor_copy, wor_bf[u], wor_a, u, 0, WA)
+
+        base = sb.tile([P, PACK, M], F32, name="base", tag="after_wor_a")
         h1 = []
         for t in range(PACK):
-            codes = sb.tile([P, P], U32, name="w1_codes%d" % t, align_bytes=64)
-            scales = sb.tile([P, P], U8, name="w1_scales%d" % t, align_bytes=64)
-            nc.vector.quantize_mx(out=codes[:].bitcast(FP8X4), scales=scales[:], in_=w1_bf[:, t, :, :].rearrange("p m j -> p (m j)"))
-            acc = ps.tile([P, J], F32, name="acc%d" % t)
-            nc.tensor.matmul_mx(out=acc[:], lhsT=codes[:].bitcast(FP8X4), lhsT_scale=scales[:], rhs=gwords[:].bitcast(FP4X4), rhs_scale=gscales[:], start=True, stop=True)
             h = sb.tile([P, J], F32, name="h1_%d" % t)
-            nc.scalar.activation(h[:], acc[:], ACT.Copy, scale=gain_sb[:, t : t + 1])
+            nc.scalar.activation(h[:], accs[t][:], ACT.Copy, scale=gain_sb[:, t : t + 1])
             h1.append(h)
 
-        wor_bf = sb.tile([P, PACK, P, PACK], BF16, name="wor_bf", align_bytes=64)
-        wor_codes = sb.tile([P, PACK, P], U32, name="wor_codes", align_bytes=64)
-        wor_scales = sb.tile([P, PACK, P], U8, name="wor_scales", align_bytes=64)
+        def pick_diff(t):
+            nc.vector.tensor_tensor(diff[t][:], h1[t][:].indirect(picks2[:]), base[:, t, :], ALU.subtract)
 
-        def quantize_wor(c):
-            half = slice(64 * c, 64 * (c + 1))
-            for t in range(PACK):
-                nc.vector.quantize_mx(out=wor_codes[:, t, half].bitcast(FP8X4), scales=wor_scales[:, t, half], in_=wor_bf[:, t, half, :].rearrange("p m j -> p (m j)"))
-
-        deal(nc.vector.tensor_copy, wor_bf, wor_raw[0], 0, 64, 0)
-        quantize_wor(0)
-
-        base = sb.tile([P, PACK, M], F32, name="base")
-        base_rs = sb.tile([P, PACK, M], F32, name="base_rs")
-        diff = sb.tile([P, PACK, M], F32, name="diff")
-        gate = sb.tile([P, PACK, M], F32, name="gate")
-        step = sb.tile([P, PACK, M], F32, name="step")
         for t in range(PACK):
             nc.vector.tensor_copy(base[:, t, :], h1[t][:].indirect(picks3[:]))
-            nc.vector.tensor_tensor(diff[:, t, :], h1[t][:].indirect(picks2[:]), base[:, t, :], ALU.subtract)
-            nc.scalar.activation(gate[:, t, :], diff[:, t, :], ACT.Sigmoid, scale=steep_sb[:, t : t + 1])
+            if t > 0:
+                pick_diff(t - 1)
+        pick_diff(PACK - 1)
+
+        gates = []
+
+        def make_gate(t, tag, align):
+            gate = sb.tile([P, M], F32, name="gate%d" % t, tag=tag, align_bytes=align)
+            nc.scalar.activation(gate[:], diff[t][:], ACT.Sigmoid, scale=steep_sb[:, t : t + 1])
+            gates.append(gate)
+
+        def scale_base(t):
             nc.scalar.activation(base_rs[:, t, :], base[:, t, :], ACT.Copy, scale=rs_sb[:, t : t + 1])
-            nc.vector.scalar_tensor_tensor(step[:, t, :], diff[:, t, :], rs_sb[:, t : t + 1], gate[:, t, :], ALU.mult, ALU.mult)
 
-        deal(nc.scalar.copy, wor_bf, wor_raw[1], 64, 96, 64)
-        deal(nc.scalar.copy, wor_bf, wor_raw[1], 96, 128, 64)
-        quantize_wor(1)
+        make_gate(0, "gate0", 32)
+        for t in range(3):
+            scale_base(t)
+        make_gate(1, "gate1", 32)
+        deal(nc.scalar.copy, wor_bf[0], wor_b, 0, WA, P)
+        scale_base(3)
+        make_gate(2, "gate2", 32)
+        make_gate(3, "after_steps", 64)
+        deal(nc.scalar.copy, wor_bf[1], wor_b, 1, WA, P)
+        for t in range(PACK):
+            nc.vector.scalar_tensor_tensor(step[:, t, :], diff[t][:], rs_sb[:, t : t + 1], gates[t][:], ALU.mult, ALU.mult)
 
+        wor_codes = sb.tile([P, PACK, P], U32, name="wor_codes", align_bytes=64)
+        wor_scales = []
+
+        def quantize_wor(t, tag):
+            scales = sb.tile([P, P], U8, name="wor_scales%d" % t, tag=tag, align_bytes=64)
+            nc.vector.quantize_mx(out=wor_codes[:, t, :].bitcast(FP8X4), scales=scales[:], in_=wor_bf[t // 2][:, t % 2, :, :].rearrange("p m j -> p (m j)"))
+            wor_scales.append(scales)
+
+        quantize_wor(0, "wor_scales0")
+        quantize_wor(1, "after_gates")
         fo_bf = sb.tile([P, M, PACK], BF16, name="fo_bf", align_bytes=64)
         nc.vector.tensor_tensor(
             fo_bf[:].rearrange("p (c i) t -> p c t i", i=4),
@@ -130,9 +156,11 @@ def tile_attend_chsoftlarger_pl_kernel(tc, tab_words, tab_scales, w1, gain, stee
             base_rs[:].rearrange("p t (c i) -> p c t i", i=4),
             ALU.add,
         )
+        quantize_wor(2, "after_steps")
         fo_codes = sb.tile([P, M], U32, name="fo_codes", align_bytes=64)
         fo_scales = sb.tile([P, M], U8, name="fo_scales", align_bytes=64)
         nc.vector.quantize_mx(out=fo_codes[:].bitcast(FP8X4), scales=fo_scales[:], in_=fo_bf[:].rearrange("p m t -> p (m t)"))
+        quantize_wor(3, "after_mix")
 
         y = sb.tile([P, PACK, M], F32, name="y")
         out_rows = out_0.rearrange("(p t) m -> p t m", t=PACK)
@@ -141,7 +169,7 @@ def tile_attend_chsoftlarger_pl_kernel(tc, tab_words, tab_scales, w1, gain, stee
             yo = ps.tile([P, 2, M], F32, name="yo%d" % u)
             for e in range(2):
                 t = 2 * u + e
-                nc.tensor.matmul_mx(out=yo[:, e, :], lhsT=wor_codes[:, t, :].bitcast(FP8X4), lhsT_scale=wor_scales[:, t, :], rhs=fo_codes[:].bitcast(FP8X4), rhs_scale=fo_scales[:], start=True, stop=True)
+                nc.tensor.matmul_mx(out=yo[:, e, :], lhsT=wor_codes[:, t, :].bitcast(FP8X4), lhsT_scale=wor_scales[t][:], rhs=fo_codes[:].bitcast(FP8X4), rhs_scale=fo_scales[:], start=True, stop=True)
             nc.vector.tensor_tensor(y[:, pair, :], yo[:], res_sb[:, pair, :], ALU.add)
             nc.sync.dma_start(out_rows[:, pair, :], y[:, pair, :])
 

from contextlib import ExitStack

import concourse.mybir as mybir

K, R, F, T, J, M = 512, 512, 512, 2048, 512, 128
FLOPS = 2 * K * R * J + 2 * R * F * M

F32 = mybir.dt.float32
BF16 = mybir.dt.bfloat16
I32 = mybir.dt.int32
U32 = mybir.dt.uint32
U16 = mybir.dt.uint16
U8 = mybir.dt.uint8
FP8X4 = mybir.dt.float8_e4m3fn_x4
FP4X4 = mybir.dt.float4_e2m1fn_x4
ACT = mybir.ActivationFunctionType
ALU = mybir.AluOpType

P = 128
PACK = 4
QUADS = 4
WA = 64


def deal(copy, grouped, raw, u, m0, m1):
    copy(
        out=grouped[:, :, m0:m1, :].rearrange("p e m j -> p m j e"),
        in_=raw[:].rearrange("p j (m t) -> p m j t", t=PACK)[:, :, :, 2 * u : 2 * u + 2],
    )


def tile_attend_chsoftlarger_pl_kernel(tc, tab_words, tab_scales, w1, gain, steep, rs, wor, res, offs, offs2, offs3, out_0, out_1, out_2):
    nc = tc.nc
    with ExitStack() as ctx:
        sb = ctx.enter_context(tc.tile_pool(name="sb", bufs=1))
        ps = ctx.enter_context(tc.psum_pool(name="ps", bufs=1))

        slots = sb.tile([P, J // 16], U16, name="slots")
        picks2 = sb.tile([P, M // 16], U16, name="picks2")
        picks3 = sb.tile([P, M // 16], U16, name="picks3")
        words = sb.tile([P, T], U16, name="words", align_bytes=64)
        tscales = sb.tile([P, T], U8, name="tscales", align_bytes=64)

        nc.vector.memset(tscales[:].bitcast(I32), 0)
        warm = sb.tile([P, 1], F32, name="warm")
        warm_out = sb.tile([P, 1], F32, name="warm_out")
        nc.vector.memset(warm[:], 0.0)
        nc.scalar.activation(warm_out[:], warm[:], ACT.Sigmoid)

        nc.sync.dma_start(slots[:], offs)
        nc.sync.dma_start(words[:].bitcast(I32), tab_words[0].bitcast(I32))
        for q in range(QUADS):
            nc.sync.dma_start(tscales[32 * q : 32 * q + 4, :].bitcast(I32), tab_scales[0, 4 * q : 4 * q + 4, :].bitcast(I32))
        w1_rows = w1.rearrange("(p j) r -> p j r", j=PACK)
        w1_raw = []
        for c in range(2):
            raw = sb.tile([P, PACK, R // 2], F32, name="w1_raw%d" % c)
            nc.sync.dma_start(raw[:], w1_rows[:, :, c * (R // 2) : (c + 1) * (R // 2)])
            w1_raw.append(raw)
        gain_sb = sb.tile([P, PACK], F32, name="gain_sb")
        steep_sb = sb.tile([P, PACK], F32, name="steep_sb", tag="after_gates", align_bytes=64)
        rs_sb = sb.tile([P, PACK], F32, name="rs_sb")
        wor_rows = wor.rearrange("(p j) f -> p j f", j=PACK)
        wor_a = sb.tile([P, PACK, PACK * WA], F32, name="wor_a", tag="after_wor_a")
        wor_b = sb.tile([P, PACK, F - PACK * WA], F32, name="wor_b")
        res_sb = sb.tile([P, PACK, M], F32, name="res_sb")
        nc.sync.dma_start(gain_sb[:], gain.rearrange("(p t) o -> p (t o)", t=PACK))
        nc.sync.dma_start(picks3[:], offs3)
        nc.sync.dma_start(picks2[:], offs2)
        nc.sync.dma_start(steep_sb[:], steep.rearrange("(p t) o -> p (t o)", t=PACK))
        nc.sync.dma_start(rs_sb[:], rs.rearrange("(p t) o -> p (t o)", t=PACK))
        nc.sync.dma_start(wor_a[:], wor_rows[:, :, : PACK * WA])
        nc.sync.dma_start(wor_b[:], wor_rows[:, :, PACK * WA :])
        nc.sync.dma_start(res_sb[:], res.rearrange("(p t) m -> p t m", t=PACK))

        gwords = sb.tile([P, J], U16, name="gwords", align_bytes=64)
        gscales = sb.tile([P, J], U8, name="gscales", align_bytes=64)
        nc.vector.tensor_copy(gwords[:], words[:].indirect(slots[:]))
        nc.vector.tensor_copy(gscales[:], tscales[:].indirect(slots[:]))

        base_rs = sb.tile([P, PACK, M], F32, name="base_rs")
        diff = [sb.tile([P, M], F32, name="diff%d" % t) for t in range(PACK)]
        step = sb.tile([P, PACK, M], F32, name="step", tag="after_mix", align_bytes=64)

        w1_bf = [sb.tile([P, 2, P, PACK], BF16, name="w1_bf%d" % u, align_bytes=64) for u in range(2)]
        w1_codes = sb.tile([P, PACK, P], U32, name="w1_codes", align_bytes=64)
        w1_scales = sb.tile([P, PACK, P], U8, name="w1_scales", align_bytes=64)
        deal(nc.scalar.copy, w1_bf[0], w1_raw[0], 0, 0, 64)
        deal(nc.scalar.copy, w1_bf[1], w1_raw[0], 1, 0, 64)
        deal(nc.vector.tensor_copy, w1_bf[0], w1_raw[1], 0, 64, 128)
        deal(nc.scalar.copy, w1_bf[1], w1_raw[1], 1, 64, 128)

        accs = []
        for t in range(PACK):
            nc.vector.quantize_mx(out=w1_codes[:, t, :].bitcast(FP8X4), scales=w1_scales[:, t, :], in_=w1_bf[t // 2][:, t % 2, :, :].rearrange("p m j -> p (m j)"))
            acc = ps.tile([P, J], F32, name="acc%d" % t)
            nc.tensor.matmul_mx(out=acc[:], lhsT=w1_codes[:, t, :].bitcast(FP8X4), lhsT_scale=w1_scales[:, t, :], rhs=gwords[:].bitcast(FP4X4), rhs_scale=gscales[:], start=True, stop=True)
            accs.append(acc)

        wor_bf = [sb.tile([P, 2, P, PACK], BF16, name="wor_bf%d" % u, align_bytes=64) for u in range(2)]
        for u in range(2):
            deal(nc.vector.tensor_copy, wor_bf[u], wor_a, u, 0, WA)

        base = sb.tile([P, PACK, M], F32, name="base", tag="after_wor_a")
        h1 = []
        for t in range(PACK):
            h = sb.tile([P, J], F32, name="h1_%d" % t)
            nc.scalar.activation(h[:], accs[t][:], ACT.Copy, scale=gain_sb[:, t : t + 1])
            h1.append(h)

        def pick_diff(t):
            nc.vector.tensor_tensor(diff[t][:], h1[t][:].indirect(picks2[:]), base[:, t, :], ALU.subtract)

        for t in range(PACK):
            nc.vector.tensor_copy(base[:, t, :], h1[t][:].indirect(picks3[:]))
            if t > 0:
                pick_diff(t - 1)
        pick_diff(PACK - 1)

        gates = []

        def make_gate(t, tag, align):
            gate = sb.tile([P, M], F32, name="gate%d" % t, tag=tag, align_bytes=align)
            nc.scalar.activation(gate[:], diff[t][:], ACT.Sigmoid, scale=steep_sb[:, t : t + 1])
            gates.append(gate)

        def scale_base(t):
            nc.scalar.activation(base_rs[:, t, :], base[:, t, :], ACT.Copy, scale=rs_sb[:, t : t + 1])

        make_gate(0, "gate0", 32)
        for t in range(3):
            scale_base(t)
        make_gate(1, "gate1", 32)
        deal(nc.scalar.copy, wor_bf[0], wor_b, 0, WA, P)
        scale_base(3)
        make_gate(2, "gate2", 32)
        make_gate(3, "after_steps", 64)
        deal(nc.scalar.copy, wor_bf[1], wor_b, 1, WA, P)
        for t in range(PACK):
            nc.vector.scalar_tensor_tensor(step[:, t, :], diff[t][:], rs_sb[:, t : t + 1], gates[t][:], ALU.mult, ALU.mult)

        wor_codes = sb.tile([P, PACK, P], U32, name="wor_codes", align_bytes=64)
        wor_scales = []

        def quantize_wor(t, tag):
            scales = sb.tile([P, P], U8, name="wor_scales%d" % t, tag=tag, align_bytes=64)
            nc.vector.quantize_mx(out=wor_codes[:, t, :].bitcast(FP8X4), scales=scales[:], in_=wor_bf[t // 2][:, t % 2, :, :].rearrange("p m j -> p (m j)"))
            wor_scales.append(scales)

        quantize_wor(0, "wor_scales0")
        quantize_wor(1, "after_gates")
        fo_bf = sb.tile([P, M, PACK], BF16, name="fo_bf", align_bytes=64)
        nc.vector.tensor_tensor(
            fo_bf[:].rearrange("p (c i) t -> p c t i", i=4),
            step[:].rearrange("p t (c i) -> p c t i", i=4),
            base_rs[:].rearrange("p t (c i) -> p c t i", i=4),
            ALU.add,
        )
        quantize_wor(2, "after_steps")
        fo_codes = sb.tile([P, M], U32, name="fo_codes", align_bytes=64)
        fo_scales = sb.tile([P, M], U8, name="fo_scales", align_bytes=64)
        nc.vector.quantize_mx(out=fo_codes[:].bitcast(FP8X4), scales=fo_scales[:], in_=fo_bf[:].rearrange("p m t -> p (m t)"))
        quantize_wor(3, "after_mix")

        y = sb.tile([P, PACK, M], F32, name="y")
        out_rows = out_0.rearrange("(p t) m -> p t m", t=PACK)
        for u in range(2):
            pair = slice(2 * u, 2 * u + 2)
            yo = ps.tile([P, 2, M], F32, name="yo%d" % u)
            for e in range(2):
                t = 2 * u + e
                nc.tensor.matmul_mx(out=yo[:, e, :], lhsT=wor_codes[:, t, :].bitcast(FP8X4), lhsT_scale=wor_scales[t][:], rhs=fo_codes[:].bitcast(FP8X4), rhs_scale=fo_scales[:], start=True, stop=True)
            nc.vector.tensor_tensor(y[:, pair, :], yo[:], res_sb[:, pair, :], ALU.add)
            nc.sync.dma_start(out_rows[:, pair, :], y[:, pair, :])

        y_bf = sb.tile([P, M, PACK], BF16, name="y_bf", align_bytes=64)
        y_codes = sb.tile([P, M], U32, name="y_codes", align_bytes=64)
        y_scales = sb.tile([P, M], U8, name="y_scales", align_bytes=64)
        halves = [slice(0, M // 2), slice(M // 2, M)]
        for half in halves:
            nc.vector.tensor_copy(y_bf[:, half, :].rearrange("p (c i) t -> p c t i", i=4), y[:, :, half].rearrange("p t (c i) -> p c t i", i=4))
        for half in halves:
            nc.vector.quantize_mx(out=y_codes[:, half].bitcast(FP8X4), scales=y_scales[:, half], in_=y_bf[:, half, :].rearrange("p m t -> p (m t)"))
        nc.scalar.dma_start(out_1[0].rearrange("p c r -> p (c r)").bitcast(I32), y_codes[:].bitcast(I32))
        for q in range(QUADS):
            queue = nc.sync if q % 2 == 0 else nc.scalar
            queue.dma_start(out_2[0, 4 * q : 4 * q + 4, :].bitcast(I32), y_scales[32 * q : 32 * q + 4, :].bitcast(I32))
